import numpy as np, ml_dtypes
CORES = [30,158,46,174,86,214]
N = 6
KB, QP = 2, 32
TAU = 16.0
def setup_inputs(rng):
    q = rng.standard_normal((N, 128, QP), dtype=np.float32) * (0.25 + np.abs(rng.standard_normal((N, 1, QP), dtype=np.float32))); k = rng.standard_normal((N, 128, KB * 128), dtype=np.float32) * (0.25 + np.abs(rng.standard_normal((N, 1, KB * 128), dtype=np.float32)))
    kn = k / np.sqrt((k ** 2).sum(axis=1, keepdims=True))
    for r in range(N):
        j = rng.integers(N, size=QP); i = rng.integers(KB * 128, size=QP)
        q[r] += rng.uniform(0, 0.8, QP).astype(np.float32) * np.sqrt((q[r] ** 2).sum(axis=0)) * kn[j, :, i].T
    return {"q": q.astype(ml_dtypes.bfloat16), "k": k.astype(ml_dtypes.bfloat16), "v": rng.standard_normal((N, 128, KB * 128), dtype=np.float32).astype(ml_dtypes.bfloat16)}
def setup_inputs_big(rng):
    d = setup_inputs(rng)
    for k in ("q", "k", "v"): d[k] = (d[k].astype(np.float32) * 1024.0).astype(d[k].dtype)
    return d
def setup_inputs_small(rng):
    d = setup_inputs(rng)
    for k in ("q", "k", "v"): d[k] = (d[k].astype(np.float32) * (1 / 1024.0)).astype(d[k].dtype)
    return d
def setup_inputs_apart(rng):
    d = setup_inputs(rng)
    f = (10.0 ** rng.permutation(np.linspace(-1.5, 1.5, N))).astype(np.float32).reshape(N, 1, 1)
    for k in ("q", "k"): d[k] = (d[k].astype(np.float32) * f).astype(d[k].dtype)
    return d
def setup_inputs_mixed(rng):
    d = setup_inputs(rng)
    for k in ("q", "k"):
        x = d[k].astype(np.float32); n = (N, 1, x.shape[2])
        f = (10.0 ** rng.uniform(-3, 3, n)).astype(np.float32); shape = rng.integers(3, size=n)
        level = np.sign(x) * np.abs(x).mean(axis=1, keepdims=True) * rng.uniform(0.9, 1.1, x.shape).astype(np.float32)
        other = x * np.where(rng.random(x.shape) < 0.75, 0.01, 1.0).astype(np.float32)
        d[k] = (np.where(shape == 1, level, np.where(shape == 2, other, x)) * f).astype(d[k].dtype)
    return d
def reference(q, k, v):
    Q, K, V = q.astype(np.float64), k.astype(np.float64), v.astype(np.float64)
    Q = Q / np.sqrt((Q ** 2).sum(axis=1, keepdims=True)); K = K / np.sqrt((K ** 2).sum(axis=1, keepdims=True))
    y = np.zeros((N, QP, 128))
    for r in range(N):
        S = TAU * np.concatenate([K[j].T @ Q[r] for j in range(N)], axis=0)
        P = np.exp(S); P = P / P.sum(axis=0)
        y[r] = P.T @ np.concatenate([V[j][:, 128 * b:128 * b + 128] for j in range(N) for b in range(KB)], axis=0)
    return {"y": y.astype(ml_dtypes.bfloat16)}

@@ -1,0 +1,232 @@
+from concourse.bass import DstId, RemoteDMATransfer
+from concourse.mybir import AluOpType, ActivationFunctionType
+
+N, QP, KB = 6, 32, 2
+W = QP + 1
+GROUPS = [[1, 2], [3, 4], [5]]
+NMAX = max(len(x) for x in GROUPS)
+NEV = 80
+
+SCRATCH = {
+    "qraw": ("sbuf", [128, QP], "bfloat16"),
+    "kk": ("sbuf", [128, KB * 128], "bfloat16"),
+    "vv": ("sbuf", [128, KB * 128], "bfloat16"),
+    "ones": ("sbuf", [128, 128], "bfloat16"),
+    "c256": ("sbuf", [128, 128], "bfloat16"),
+    "ident": ("sbuf", [128, 128], "bfloat16"),
+    "mask": ("sbuf", [128, 4], "float32"),
+    "qsq": ("sbuf", [128, QP], "bfloat16"),
+    "sq": ("sbuf", [128, QP], "float32"),
+    "rx": ("sbuf", [128, QP], "float32"),
+    "u": ("sbuf", [128, QP], "float32"),
+    "qown": ("sbuf", [128, QP], "bfloat16"),
+    "qall": ("sbuf", [128, (N - 1) * QP], "bfloat16"),
+    "ksq": ("sbuf", [128, KB * 128], "bfloat16"),
+    "sk": ("sbuf", [128, KB], "float32"),
+    "rk": ("sbuf", [128, KB], "float32"),
+    "P": ("sbuf", [128, KB, N * QP], "bfloat16"),
+    "msg": ("sbuf", [128, N - 1, W], "bfloat16"),
+    "land": ("sbuf", [128, N - 1, W], "bfloat16"),
+    "rden": ("sbuf", [128, 1], "float32"),
+    "yt": ("sbuf", [128, 128], "bfloat16"),
+}
+for _b in range(8):
+    SCRATCH["ps%d" % _b] = ("psum", [128, 512], "float32")
+
+SEMAPHORES = (["qs%d" % j for j in range(N)] + ["ps%d" % p for p in range(1, N)] + ["sent"]
+              + ["e%d" % i for i in range(NEV)])
+
+
+def rank_program(g, core, T, topo):
+    rank = T.rank_of(core)
+    if rank is None:
+        return
+    ACT, OP = ActivationFunctionType, AluOpType
+    Q = {"g": g, "v": g.vector, "s": g.scalar, "t": g.tensor, "y": g.sync}
+    cnt, seen = [0], {}
+
+    def ev():
+        cnt[0] += 1
+        return "e%d" % (cnt[0] - 1)
+
+    def wait(qn, name, val=1):
+        if seen.get((qn, name), 0) < val:
+            seen[(qn, name)] = val
+            Q[qn].wait_ge(T.sem[name], val)
+
+    def engines(src):
+        m = None
+        for d in T.cores:
+            if d != src:
+                m = topo.mask(src, d) if m is None else m & topo.mask(src, d)
+        return [e for e in range(m.bit_length()) if (m >> e) & 1]
+
+    def share(n, src):
+        k = 1
+        while 2 * k * n <= len(engines(src)):
+            k *= 2
+        return k
+
+    def bits(es):
+        m = 0
+        for e in es:
+            m |= 1 << e
+        return m
+
+    PS = [T["ps%d" % b] for b in range(8)]
+    readers = {b: [] for b in range(8)}
+
+    def claim(b):
+        for n_, v_ in readers[b]:
+            wait("t", n_, v_)
+        readers[b] = []
+        return PS[b]
+
+    ldq, ldk, ldv = ev(), ev(), ev()
+    g.sync.dma_start(T.qraw[:, :], T.q[:, :]).then_inc(T.sem[ldq], 16)
+    g.sync.dma_start(T.kk[:, :], T.k[:, :]).then_inc(T.sem[ldk], 16)
+    g.sync.dma_start(T.vv[:, :], T.v[:, :]).then_inc(T.sem[ldv], 16)
+
+    init, ninit = ev(), [0]
+
+    def fill(ap, c):
+        g.vector.memset(ap, c).then_inc(T.sem[init], 1)
+        ninit[0] += 1
+
+    fill(T.c256[:, :], 1.0 / 256.0)
+    fill(T.ones[:, :], 1.0)
+    fill(T.msg[:, :, :], 0.0)
+    for i in range(NMAX):
+        for j in range(NMAX):
+            fill(T.mask[32 * i:32 * i + 32, j:j + 1], 1.0 if i == j else 0.0)
+    NI = ninit[0]
+    eid = ev()
+    wait("g", init, NI)
+    g.affine_select(T.ident[:, :], T.ones[:, :], [[-1, 128]], OP.is_equal, 0.0, 0, 1).then_inc(T.sem[eid], 1)
+
+    eqsq, exa, exb, esq, erx, eu, eqn = ev(), ev(), ev(), ev(), ev(), ev(), ev()
+    wait("v", init, NI)
+    wait("v", ldq, 16)
+    g.vector.tensor_tensor(T.qsq[:, :], T.qraw[:, :], T.qraw[:, :], OP.mult).then_inc(T.sem[eqsq], 1)
+    wait("t", init, NI)
+    wait("t", eqsq)
+    g.tensor.matmul(PS[0][:, 0:QP], T.c256[:, :], T.qsq[:, :], True, True).then_inc(T.sem[exa], 1)
+    g.tensor.matmul(PS[1][:, 0:QP], T.c256[:, :], T.qsq[:, :], True, True).then_inc(T.sem[exb], 1)
+    wait("s", exa)
+    g.scalar.activation(T.sq[:, :], PS[0][:, 0:QP], ACT.Sqrt).then_inc(T.sem[esq], 1)
+    readers[0].append((esq, 1))
+    wait("v", exb)
+    g.vector.reciprocal(T.rx[:, :], PS[1][:, 0:QP]).then_inc(T.sem[erx], 1)
+    readers[1].append((erx, 1))
+    wait("v", erx)
+    g.vector.tensor_tensor(T.u[:, :], T.qraw[:, :], T.rx[:, :], OP.mult).then_inc(T.sem[eu], 1)
+    wait("v", eu)
+    wait("v", esq)
+    g.vector.tensor_tensor(T.qown[:, :], T.u[:, :], T.sq[:, :], OP.mult).then_inc(T.sem[eqn], 1)
+
+    my = engines(core)
+    sent = 0
+    ids, dsts = [], []
+    for p in range(1, N):
+        rid, pid = topo.addr(T.cores[(rank + p) % N], core)
+        ids.append(DstId(rid=rid, pnc=pid))
+        dsts.append(T.qall[:, QP * (p - 1):QP * p])
+    wait("g", eqn)
+    g.remote_dma_fused([RemoteDMATransfer(dst_ids=ids, dma_engine_mask=bits(my), remote_sem=T.sem["qs%d" % rank],
+                                          srcs=[T.qown[:, :]], dsts=dsts)], local_sem=T.sem.sent)
+    sent += len(my)
+
+    eksq, exk, esk, erk = ev(), ev(), ev(), ev()
+    wait("s", ldk, 16)
+    g.scalar.activation(T.ksq[:, :], T.kk[:, :], ACT.Square).then_inc(T.sem[eksq], 1)
+    eS = [ev(), ev()]
+    eE = [ev(), ev()]
+    wait("t", eqn)
+    wait("t", ldk, 16)
+    for b in range(KB):
+        g.tensor.matmul(PS[4 + b][:, 0:QP], T.kk[:, 128 * b:128 * b + 128], T.qown[:, :], True, True).then_inc(T.sem[eS[b]], 1)
+    wait("t", eksq)
+    for b in range(KB):
+        g.tensor.matmul(PS[2][:, b:b + 1], T.ksq[:, 128 * b:128 * b + 128], T.ones[:, 0:1], True, True).then_inc(T.sem[exk], 1)
+    wait("s", exk, KB)
+    g.scalar.activation(T.sk[:, :], PS[2][:, 0:KB], ACT.Sqrt).then_inc(T.sem[esk], 1)
+    readers[2].append((esk, 1))
+    wait("v", esk)
+    g.vector.reciprocal(T.rk[:, :], T.sk[:, :]).then_inc(T.sem[erk], 1)
+    wait("s", erk)
+    for b in range(KB):
+        wait("s", eS[b])
+        g.scalar.activation(T.P[:, b, 0:QP], PS[4 + b][:, 0:QP], ACT.Exp, bias=-16.0,
+                            scale=T.rk[:, b:b + 1]).then_inc(T.sem[eE[b]], 1)
+        readers[4 + b].append((eE[b], 1))
+    eown = eE
+
+    wait("t", ldv, 16)
+    for gi, grp in enumerate(GROUPS):
+        n, p0 = len(grp), grp[0]
+        w = QP * n
+        base = 4 * (gi % 2)
+        for p in grp:
+            j = (rank - p) % N
+            wait("t", "qs%d" % j, len(engines(T.cores[j])))
+        eS, eE = [ev(), ev()], [ev(), ev()]
+        enum, eden, ecn, ecd = ev(), ev(), ev(), ev()
+        for b in range(KB):
+            S = claim(base + b)
+            g.tensor.matmul(S[:, 0:w], T.kk[:, 128 * b:128 * b + 128], T.qall[:, QP * (p0 - 1):QP * (p0 - 1) + w],
+                            True, True).then_inc(T.sem[eS[b]], 1)
+        for b in range(KB):
+            wait("s", eS[b])
+            g.scalar.activation(T.P[:, b, QP * p0:QP * p0 + w], PS[base + b][:, 0:w], ACT.Exp, bias=-16.0,
+                                scale=T.rk[:, b:b + 1]).then_inc(T.sem[eE[b]], 1)
+            readers[base + b].append((eE[b], 1))
+        NUM, DEN = claim(base + 2), claim(base + 3)
+        for b in range(KB):
+            wait("t", eE[b])
+            Pb = T.P[:, b, QP * p0:QP * p0 + w]
+            g.tensor.matmul(NUM[:, 0:w], T.vv[:, 128 * b:128 * b + 128], Pb, b == 0, b == KB - 1).then_inc(T.sem[enum], 1)
+            g.tensor.matmul(DEN[0:w, 0:1], Pb, T.ones[:, 0:1], b == 0, b == KB - 1).then_inc(T.sem[eden], 1)
+        wait("v", enum, KB)
+        out = T.msg[:, p0 - 1, 0:QP] if n == 1 else T.msg[:, p0 - 1:p0 - 1 + n, 0:QP]
+        g.vector.tensor_copy(out, NUM[:, 0:w]).then_inc(T.sem[ecn], 1)
+        readers[base + 2].append((ecn, 1))
+        wait("v", eden, KB)
+        g.vector.tensor_scalar(T.msg[0:w, p0 - 1:p0 - 1 + n, QP], T.mask[0:w, 0:n], DEN[0:w, 0:1], None,
+                               OP.mult).then_inc(T.sem[ecd], 1)
+        readers[base + 3].append((ecd, 1))
+        k = share(n, core)
+        trs = []
+        for i, p in enumerate(grp):
+            rid, pid = topo.addr(T.cores[(rank - p) % N], core)
+            trs.append(RemoteDMATransfer(dst_ids=[DstId(rid=rid, pnc=pid)], dma_engine_mask=bits(my[i * k:(i + 1) * k]),
+                                         remote_sem=T.sem["ps%d" % p], srcs=[T.msg[:, p - 1, :]],
+                                         dsts=[T.land[:, p - 1, :]]))
+            sent += k
+        wait("g", ecn)
+        wait("g", ecd)
+        g.remote_dma_fused(trs, local_sem=T.sem.sent)
+
+    base = 4 * (len(GROUPS) % 2)
+    YA, DA = claim(base), claim(base + 1)
+    ey, ed, erd, eyt, est = ev(), ev(), ev(), ev(), ev()
+    for b in range(KB):
+        wait("t", eown[b])
+        g.tensor.matmul(DA[0:QP, 0:1], T.P[:, b, 0:QP], T.ones[:, 0:1], b == 0, False).then_inc(T.sem[ed], 1)
+        g.tensor.matmul(YA[0:QP, 0:128], T.P[:, b, 0:QP], T.vv[:, 128 * b:128 * b + 128], b == 0, False).then_inc(T.sem[ey], 1)
+    wait("t", eid)
+    order = [(p, i, len(grp)) for grp in GROUPS for i, p in enumerate(grp)]
+    for c, (p, i, n) in enumerate(order):
+        last = c == len(order) - 1
+        wait("t", "ps%d" % p, share(n, T.cores[(rank + p) % N]))
+        g.tensor.matmul(DA[0:QP, 0:1], T.ident[:, QP * i:QP * i + QP], T.land[:, p - 1, QP:QP + 1], False,
+                        last).then_inc(T.sem[ed], 1)
+        g.tensor.matmul(YA[0:QP, 0:128], T.land[:, p - 1, 0:QP], T.ident[:, :], False, last).then_inc(T.sem[ey], 1)
+    wait("v", ed, KB + N - 1)
+    g.vector.reciprocal(T.rden[0:QP, :], DA[0:QP, 0:1]).then_inc(T.sem[erd], 1)
+    wait("v", erd)
+    wait("v", ey, KB + N - 1)
+    g.vector.tensor_scalar(T.yt[0:QP, :], YA[0:QP, 0:128], T.rden[0:QP, 0:1], None, OP.mult).then_inc(T.sem[eyt], 1)
+    wait("y", eyt)
+    g.sync.dma_start(T.y[:, :], T.yt[0:QP, :]).then_inc(T.sem[est], 16)
+    wait("y", est, 16)
+    wait("g", "sent", sent)

@@ -93,14 +93,17 @@ def rank_program(g, core, T, topo):
         g.vector.memset(ap, c).then_inc(T.sem[init], 1)
         ninit[0] += 1
 
+    eone, ezero = ev(), ev()
+    g.vector.memset(T.ones[:, :], 1.0).then_inc(T.sem[eone], 1)
     fill(T.c256[:, :], 1.0 / 256.0)
-    fill(T.ones[:, :], 1.0)
-    fill(T.msg[:, :, :], 0.0)
+    wait("s", eone)
+    g.scalar.activation(T.msg[:, :, QP], T.ones[:, 0:N - 1], ACT.Sqrt, scale=0.0).then_inc(T.sem[ezero], 1)
     for i in range(NMAX):
         for j in range(NMAX):
             fill(T.mask[32 * i:32 * i + 32, j:j + 1], 1.0 if i == j else 0.0)
     NI = ninit[0]
     eid = ev()
+    wait("g", eone)
     wait("g", init, NI)
     g.affine_select(T.ident[:, :], T.ones[:, :], [[-1, 128]], OP.is_equal, 0.0, 0, 1).then_inc(T.sem[eid], 1)
 
@@ -109,6 +112,7 @@ def rank_program(g, core, T, topo):
     wait("v", ldq, 16)
     g.vector.tensor_tensor(T.qsq[:, :], T.qraw[:, :], T.qraw[:, :], OP.mult).then_inc(T.sem[eqsq], 1)
     wait("t", init, NI)
+    wait("t", eone)
     wait("t", eqsq)
     g.tensor.matmul(PS[0][:, 0:QP], T.c256[:, :], T.qsq[:, :], True, True).then_inc(T.sem[exa], 1)
     g.tensor.matmul(PS[1][:, 0:QP], T.c256[:, :], T.qsq[:, :], True, True).then_inc(T.sem[exb], 1)
@@ -191,6 +195,7 @@ def rank_program(g, core, T, topo):
         g.vector.tensor_copy(out, NUM[:, 0:w]).then_inc(T.sem[ecn], 1)
         readers[base + 2].append((ecn, 1))
         wait("v", eden, KB)
+        wait("v", ezero)
         g.vector.tensor_scalar(T.msg[0:w, p0 - 1:p0 - 1 + n, QP], T.mask[0:w, 0:n], DEN[0:w, 0:1], None,
                                OP.mult).then_inc(T.sem[ecd], 1)
         readers[base + 3].append((ecd, 1))

@@ -5,13 +5,17 @@ N, QP, KB = 6, 32, 2
 W = QP + 1
 GROUPS = [[1, 2], [3, 4], [5]]
 NMAX = max(len(x) for x in GROUPS)
-NEV = 80
+RAW = N - 1
+NEV = 120
 
 SCRATCH = {
     "qraw": ("sbuf", [128, QP], "bfloat16"),
+    "qd": ("dram", [128, QP], "bfloat16"),
+    "ql": ("dram", [128, QP], "bfloat16"),
     "kk": ("sbuf", [128, KB * 128], "bfloat16"),
     "vv": ("sbuf", [128, KB * 128], "bfloat16"),
     "ones": ("sbuf", [128, 128], "bfloat16"),
+    "onec": ("sbuf", [128, 1], "bfloat16"),
     "c256": ("sbuf", [128, 128], "bfloat16"),
     "ident": ("sbuf", [128, 128], "bfloat16"),
     "mask": ("sbuf", [128, 4], "float32"),
@@ -20,10 +24,13 @@ SCRATCH = {
     "rx": ("sbuf", [128, QP], "float32"),
     "u": ("sbuf", [128, QP], "float32"),
     "qown": ("sbuf", [128, QP], "bfloat16"),
+    "sc": ("sbuf", [128, QP], "bfloat16"),
+    "scl": ("sbuf", [128, QP], "bfloat16"),
     "qall": ("sbuf", [128, (N - 1) * QP], "bfloat16"),
     "ksq": ("sbuf", [128, KB * 128], "bfloat16"),
     "sk": ("sbuf", [128, KB], "float32"),
     "rk": ("sbuf", [128, KB], "float32"),
+    "Ssc": ("sbuf", [128, KB, QP], "float32"),
     "P": ("sbuf", [128, KB, N * QP], "bfloat16"),
     "msg": ("sbuf", [128, N - 1, W], "bfloat16"),
     "land": ("sbuf", [128, N - 1, W], "bfloat16"),
@@ -33,8 +40,43 @@ SCRATCH = {
 for _b in range(8):
     SCRATCH["ps%d" % _b] = ("psum", [128, 512], "float32")
 
-SEMAPHORES = (["qs%d" % j for j in range(N)] + ["ps%d" % p for p in range(1, N)] + ["sent"]
-              + ["e%d" % i for i in range(NEV)])
+SEMAPHORES = (["qs%d" % j for j in range(N)] + ["rw%d" % j for j in range(N)] + ["ps%d" % p for p in range(1, N)]
+              + ["sent"] + ["e%d" % i for i in range(NEV)])
+
+
+def rounds_of(T, topo):
+    def matchings(rem):
+        if not rem:
+            return [[]]
+        a, out = rem[0], []
+        for b in rem[1:]:
+            for m in matchings([x for x in rem if x != a and x != b]):
+                out.append([(a, b)] + m)
+        return out
+
+    def far(m):
+        return sum(0 if topo.same_plane(T.cores[a], T.cores[b]) else 1 for a, b in m)
+
+    allm = sorted(matchings(list(range(N))), key=far)
+
+    def pick(chosen, used):
+        if len(chosen) == N - 1:
+            return chosen
+        for m in allm:
+            if not any(e in used for e in m):
+                r = pick(chosen + [m], used | set(m))
+                if r:
+                    return r
+        return None
+
+    chosen = sorted(pick([], set()), key=lambda m: -far(m))
+    part = {}
+    for t, m in enumerate(chosen):
+        part[t + 1] = {}
+        for a, b in m:
+            part[t + 1][a] = b
+            part[t + 1][b] = a
+    return part
 
 
 def rank_program(g, core, T, topo):
@@ -44,6 +86,7 @@ def rank_program(g, core, T, topo):
     ACT, OP = ActivationFunctionType, AluOpType
     Q = {"g": g, "v": g.vector, "s": g.scalar, "t": g.tensor, "y": g.sync}
     cnt, seen = [0], {}
+    part = rounds_of(T, topo)
 
     def ev():
         cnt[0] += 1
@@ -82,8 +125,9 @@ def rank_program(g, core, T, topo):
         readers[b] = []
         return PS[b]
 
-    ldq, ldk, ldv = ev(), ev(), ev()
+    ldq, ldd, ldk, ldv = ev(), ev(), ev(), ev()
     g.sync.dma_start(T.qraw[:, :], T.q[:, :]).then_inc(T.sem[ldq], 16)
+    g.scalar.dma_start(T.qd[:, :], T.q[:, :]).then_inc(T.sem[ldd], 16)
     g.sync.dma_start(T.kk[:, :], T.k[:, :]).then_inc(T.sem[ldk], 16)
     g.sync.dma_start(T.vv[:, :], T.v[:, :]).then_inc(T.sem[ldv], 16)
 
@@ -102,12 +146,19 @@ def rank_program(g, core, T, topo):
         for j in range(NMAX):
             fill(T.mask[32 * i:32 * i + 32, j:j + 1], 1.0 if i == j else 0.0)
     NI = ninit[0]
-    eid = ev()
-    wait("g", eone)
-    wait("g", init, NI)
-    g.affine_select(T.ident[:, :], T.ones[:, :], [[-1, 128]], OP.is_equal, 0.0, 0, 1).then_inc(T.sem[eid], 1)
 
-    eqsq, exa, exb, esq, erx, eu, eqn = ev(), ev(), ev(), ev(), ev(), ev(), ev()
+    my = engines(core)
+    sent = 0
+    ids = {}
+    for t in range(1, N):
+        rid, pid = topo.addr(T.cores[part[t][rank]], core)
+        ids[t] = DstId(rid=rid, pnc=pid)
+    wait("g", ldd, 16)
+    g.remote_dma_fused([RemoteDMATransfer(dst_ids=[ids[RAW]], dma_engine_mask=bits(my), remote_sem=T.sem["rw%d" % rank],
+                                          srcs=[T.qd[:, :]], dsts=[T.ql[:, :]])], local_sem=T.sem.sent)
+    sent += len(my)
+
+    eqsq, exa, exb, esq, erx, eu, eqn, esc = ev(), ev(), ev(), ev(), ev(), ev(), ev(), ev()
     wait("v", init, NI)
     wait("v", ldq, 16)
     g.vector.tensor_tensor(T.qsq[:, :], T.qraw[:, :], T.qraw[:, :], OP.mult).then_inc(T.sem[eqsq], 1)
@@ -127,24 +178,31 @@ def rank_program(g, core, T, topo):
     wait("v", eu)
     wait("v", esq)
     g.vector.tensor_tensor(T.qown[:, :], T.u[:, :], T.sq[:, :], OP.mult).then_inc(T.sem[eqn], 1)
+    g.vector.tensor_tensor(T.sc[:, :], T.rx[:, :], T.sq[:, :], OP.mult).then_inc(T.sem[esc], 1)
 
-    my = engines(core)
-    sent = 0
-    ids, dsts = [], []
-    for p in range(1, N):
-        rid, pid = topo.addr(T.cores[(rank + p) % N], core)
-        ids.append(DstId(rid=rid, pnc=pid))
-        dsts.append(T.qall[:, QP * (p - 1):QP * p])
+    early = [t for t in range(1, N) if t != RAW]
     wait("g", eqn)
-    g.remote_dma_fused([RemoteDMATransfer(dst_ids=ids, dma_engine_mask=bits(my), remote_sem=T.sem["qs%d" % rank],
-                                          srcs=[T.qown[:, :]], dsts=dsts)], local_sem=T.sem.sent)
+    g.remote_dma_fused([RemoteDMATransfer(dst_ids=[ids[t] for t in early], dma_engine_mask=bits(my),
+                                          remote_sem=T.sem["qs%d" % rank], srcs=[T.qown[:, :]],
+                                          dsts=[T.qall[:, QP * (t - 1):QP * t] for t in early])], local_sem=T.sem.sent)
     sent += len(my)
+    wait("g", esc)
+    g.remote_dma_fused([RemoteDMATransfer(dst_ids=[ids[RAW]], dma_engine_mask=bits(my), remote_sem=T.sem["qs%d" % rank],
+                                          srcs=[T.sc[:, :]], dsts=[T.scl[:, :]])], local_sem=T.sem.sent)
+    sent += len(my)
+    eid = ev()
+    wait("g", eone)
+    g.affine_select(T.ident[:, :], T.ones[:, :], [[-1, 128]], OP.is_equal, 0.0, 0, 1).then_inc(T.sem[eid], 1)
 
-    eksq, exk, esk, erk = ev(), ev(), ev(), ev()
+    jr = part[RAW][rank]
+    eld = ev()
+    wait("y", "rw%d" % jr, len(engines(T.cores[jr])))
+    g.sync.dma_start(T.qall[:, QP * (RAW - 1):QP * RAW], T.ql[:, :]).then_inc(T.sem[eld], 16)
+
+    eksq, exk, esk, erk, eexp = ev(), ev(), ev(), ev(), ev()
     wait("s", ldk, 16)
     g.scalar.activation(T.ksq[:, :], T.kk[:, :], ACT.Square).then_inc(T.sem[eksq], 1)
-    eS = [ev(), ev()]
-    eE = [ev(), ev()]
+    eS, eE = [ev(), ev()], [ev(), ev()]
     wait("t", eqn)
     wait("t", ldk, 16)
     for b in range(KB):
@@ -155,6 +213,7 @@ def rank_program(g, core, T, topo):
     wait("s", exk, KB)
     g.scalar.activation(T.sk[:, :], PS[2][:, 0:KB], ACT.Sqrt).then_inc(T.sem[esk], 1)
     readers[2].append((esk, 1))
+    g.scalar.activation(T.onec[:, :], T.ones[:, 0:1], ACT.Exp, scale=0.0).then_inc(T.sem[eexp], 1)
     wait("v", esk)
     g.vector.reciprocal(T.rk[:, :], T.sk[:, :]).then_inc(T.sem[erk], 1)
     wait("s", erk)
@@ -166,72 +225,122 @@ def rank_program(g, core, T, topo):
     eown = eE
 
     wait("t", ldv, 16)
-    for gi, grp in enumerate(GROUPS):
+    wait("t", eexp)
+    st = {}
+
+    def scores(gi):
+        grp = GROUPS[gi]
         n, p0 = len(grp), grp[0]
         w = QP * n
         base = 4 * (gi % 2)
-        for p in grp:
-            j = (rank - p) % N
-            wait("t", "qs%d" % j, len(engines(T.cores[j])))
+        raw = grp == [RAW]
+        if raw:
+            wait("t", eld, 16)
+        else:
+            for p in grp:
+                j = part[p][rank]
+                wait("t", "qs%d" % j, len(engines(T.cores[j])))
         eS, eE = [ev(), ev()], [ev(), ev()]
-        enum, eden, ecn, ecd = ev(), ev(), ev(), ev()
         for b in range(KB):
             S = claim(base + b)
             g.tensor.matmul(S[:, 0:w], T.kk[:, 128 * b:128 * b + 128], T.qall[:, QP * (p0 - 1):QP * (p0 - 1) + w],
                             True, True).then_inc(T.sem[eS[b]], 1)
+        eM = [ev(), ev()] if raw else None
+        if raw:
+            wait("v", "qs%d" % jr, len(engines(T.cores[jr])))
+            for b in range(KB):
+                wait("v", eS[b])
+                g.vector.tensor_tensor(T.Ssc[:, b, :], PS[base + b][:, 0:w], T.scl[:, :], OP.mult).then_inc(T.sem[eM[b]], 1)
+                readers[base + b].append((eM[b], 1))
         for b in range(KB):
-            wait("s", eS[b])
-            g.scalar.activation(T.P[:, b, QP * p0:QP * p0 + w], PS[base + b][:, 0:w], ACT.Exp, bias=-16.0,
+            if raw:
+                wait("s", eM[b])
+                src = T.Ssc[:, b, :]
+            else:
+                wait("s", eS[b])
+                src = PS[base + b][:, 0:w]
+            g.scalar.activation(T.P[:, b, QP * p0:QP * p0 + w], src, ACT.Exp, bias=-16.0,
                                 scale=T.rk[:, b:b + 1]).then_inc(T.sem[eE[b]], 1)
-            readers[base + b].append((eE[b], 1))
+            if not raw:
+                readers[base + b].append((eE[b], 1))
+        st[gi] = eE
+
+    def parts(gi):
+        grp = GROUPS[gi]
+        n, p0 = len(grp), grp[0]
+        w = QP * n
+        base = 4 * (gi % 2)
+        eE = st[gi]
+        enum, eden, ecn, ecd = ev(), ev(), ev(), ev()
         NUM, DEN = claim(base + 2), claim(base + 3)
         for b in range(KB):
             wait("t", eE[b])
             Pb = T.P[:, b, QP * p0:QP * p0 + w]
+            g.tensor.matmul(DEN[0:w, 0:1], Pb, T.onec[:, 0:1], b == 0, b == KB - 1).then_inc(T.sem[eden], 1)
             g.tensor.matmul(NUM[:, 0:w], T.vv[:, 128 * b:128 * b + 128], Pb, b == 0, b == KB - 1).then_inc(T.sem[enum], 1)
-            g.tensor.matmul(DEN[0:w, 0:1], Pb, T.ones[:, 0:1], b == 0, b == KB - 1).then_inc(T.sem[eden], 1)
+        if n == 1:
+            wait("s", eden, KB)
+            wait("s", ezero)
+            g.scalar.activation(T.msg[0:QP, p0 - 1, QP:QP + 1], DEN[0:QP, 0:1], ACT.Copy).then_inc(T.sem[ecd], 1)
         wait("v", enum, KB)
         out = T.msg[:, p0 - 1, 0:QP] if n == 1 else T.msg[:, p0 - 1:p0 - 1 + n, 0:QP]
         g.vector.tensor_copy(out, NUM[:, 0:w]).then_inc(T.sem[ecn], 1)
         readers[base + 2].append((ecn, 1))
-        wait("v", eden, KB)
-        wait("v", ezero)
-        g.vector.tensor_scalar(T.msg[0:w, p0 - 1:p0 - 1 + n, QP], T.mask[0:w, 0:n], DEN[0:w, 0:1], None,
-                               OP.mult).then_inc(T.sem[ecd], 1)
+        if n > 1:
+            wait("v", eden, KB)
+            wait("v", ezero)
+            g.vector.tensor_scalar(T.msg[0:w, p0 - 1:p0 - 1 + n, QP], T.mask[0:w, 0:n], DEN[0:w, 0:1], None,
+                                   OP.mult).then_inc(T.sem[ecd], 1)
         readers[base + 3].append((ecd, 1))
         k = share(n, core)
         trs = []
         for i, p in enumerate(grp):
-            rid, pid = topo.addr(T.cores[(rank - p) % N], core)
-            trs.append(RemoteDMATransfer(dst_ids=[DstId(rid=rid, pnc=pid)], dma_engine_mask=bits(my[i * k:(i + 1) * k]),
+            trs.append(RemoteDMATransfer(dst_ids=[ids[p]], dma_engine_mask=bits(my[i * k:(i + 1) * k]),
                                          remote_sem=T.sem["ps%d" % p], srcs=[T.msg[:, p - 1, :]],
                                          dsts=[T.land[:, p - 1, :]]))
-            sent += k
         wait("g", ecn)
         wait("g", ecd)
         g.remote_dma_fused(trs, local_sem=T.sem.sent)
+        return k * n
+
+    NG = len(GROUPS)
+    for gi in range(NG - 2):
+        scores(gi)
+        sent += parts(gi)
+    scores(NG - 2)
+    scores(NG - 1)
+    sent += parts(NG - 2)
+    sent += parts(NG - 1)
 
     base = 4 * (len(GROUPS) % 2)
-    YA, DA = claim(base), claim(base + 1)
-    ey, ed, erd, eyt, est = ev(), ev(), ev(), ev(), ev()
+    H = 64
+    YA, DA = [claim(base), claim(base + 2)], claim(base + 1)
+    ey, ed, erd, eyt, est = [ev(), ev()], ev(), ev(), ev(), ev()
     for b in range(KB):
         wait("t", eown[b])
-        g.tensor.matmul(DA[0:QP, 0:1], T.P[:, b, 0:QP], T.ones[:, 0:1], b == 0, False).then_inc(T.sem[ed], 1)
-        g.tensor.matmul(YA[0:QP, 0:128], T.P[:, b, 0:QP], T.vv[:, 128 * b:128 * b + 128], b == 0, False).then_inc(T.sem[ey], 1)
+        g.tensor.matmul(DA[0:QP, 0:1], T.P[:, b, 0:QP], T.onec[:, 0:1], b == 0, False).then_inc(T.sem[ed], 1)
+        for h in range(2):
+            g.tensor.matmul(YA[h][0:QP, 0:H], T.P[:, b, 0:QP], T.vv[:, 128 * b + H * h:128 * b + H * h + H], b == 0,
+                            False).then_inc(T.sem[ey[h]], 1)
     wait("t", eid)
     order = [(p, i, len(grp)) for grp in GROUPS for i, p in enumerate(grp)]
     for c, (p, i, n) in enumerate(order):
         last = c == len(order) - 1
-        wait("t", "ps%d" % p, share(n, T.cores[(rank + p) % N]))
+        wait("t", "ps%d" % p, share(n, T.cores[part[p][rank]]))
         g.tensor.matmul(DA[0:QP, 0:1], T.ident[:, QP * i:QP * i + QP], T.land[:, p - 1, QP:QP + 1], False,
                         last).then_inc(T.sem[ed], 1)
-        g.tensor.matmul(YA[0:QP, 0:128], T.land[:, p - 1, 0:QP], T.ident[:, :], False, last).then_inc(T.sem[ey], 1)
+        for h in range(2):
+            g.tensor.matmul(YA[h][0:QP, 0:H], T.land[:, p - 1, 0:QP], T.ident[:, H * h:H * h + H], False,
+                            last).then_inc(T.sem[ey[h]], 1)
     wait("v", ed, KB + N - 1)
     g.vector.reciprocal(T.rden[0:QP, :], DA[0:QP, 0:1]).then_inc(T.sem[erd], 1)
     wait("v", erd)
-    wait("v", ey, KB + N - 1)
-    g.vector.tensor_scalar(T.yt[0:QP, :], YA[0:QP, 0:128], T.rden[0:QP, 0:1], None, OP.mult).then_inc(T.sem[eyt], 1)
-    wait("y", eyt)
+    wait("v", ey[0], KB + N - 1)
+    g.vector.tensor_scalar(T.yt[0:QP, 0:H], YA[0][0:QP, 0:H], T.rden[0:QP, 0:1], None, OP.mult).then_inc(T.sem[eyt], 1)
+    wait("s", erd)
+    wait("s", ey[1], KB + N - 1)
+    g.scalar.activation(T.yt[0:QP, H:2 * H], YA[1][0:QP, 0:H], ACT.Copy, scale=T.rden[0:QP, 0:1]).then_inc(T.sem[eyt], 1)
+    wait("y", eyt, 2)
     g.sync.dma_start(T.y[:, :], T.yt[0:QP, :]).then_inc(T.sem[est], 16)
     wait("y", est, 16)
     wait("g", "sent", sent)

from concourse.bass import DstId, RemoteDMATransfer
from concourse.mybir import AluOpType, ActivationFunctionType

N, QP, KB = 6, 32, 2
W = QP + 1
GROUPS = [[1, 2], [3, 4], [5]]
NMAX = max(len(x) for x in GROUPS)
RAW = N - 1
NEV = 120

SCRATCH = {
    "qraw": ("sbuf", [128, QP], "bfloat16"),
    "qd": ("dram", [128, QP], "bfloat16"),
    "ql": ("dram", [128, QP], "bfloat16"),
    "kk": ("sbuf", [128, KB * 128], "bfloat16"),
    "vv": ("sbuf", [128, KB * 128], "bfloat16"),
    "ones": ("sbuf", [128, 128], "bfloat16"),
    "onec": ("sbuf", [128, 1], "bfloat16"),
    "c256": ("sbuf", [128, 128], "bfloat16"),
    "ident": ("sbuf", [128, 128], "bfloat16"),
    "mask": ("sbuf", [128, 4], "float32"),
    "qsq": ("sbuf", [128, QP], "bfloat16"),
    "sq": ("sbuf", [128, QP], "float32"),
    "rx": ("sbuf", [128, QP], "float32"),
    "u": ("sbuf", [128, QP], "float32"),
    "qown": ("sbuf", [128, QP], "bfloat16"),
    "sc": ("sbuf", [128, QP], "bfloat16"),
    "scl": ("sbuf", [128, QP], "bfloat16"),
    "qall": ("sbuf", [128, (N - 1) * QP], "bfloat16"),
    "ksq": ("sbuf", [128, KB * 128], "bfloat16"),
    "sk": ("sbuf", [128, KB], "float32"),
    "rk": ("sbuf", [128, KB], "float32"),
    "Ssc": ("sbuf", [128, KB, QP], "float32"),
    "P": ("sbuf", [128, KB, N * QP], "bfloat16"),
    "msg": ("sbuf", [128, N - 1, W], "bfloat16"),
    "land": ("sbuf", [128, N - 1, W], "bfloat16"),
    "rden": ("sbuf", [128, 1], "float32"),
    "yt": ("sbuf", [128, 128], "bfloat16"),
}
for _b in range(8):
    SCRATCH["ps%d" % _b] = ("psum", [128, 512], "float32")

SEMAPHORES = (["qs%d" % j for j in range(N)] + ["rw%d" % j for j in range(N)] + ["ps%d" % p for p in range(1, N)]
              + ["sent"] + ["e%d" % i for i in range(NEV)])


def rounds_of(T, topo):
    def matchings(rem):
        if not rem:
            return [[]]
        a, out = rem[0], []
        for b in rem[1:]:
            for m in matchings([x for x in rem if x != a and x != b]):
                out.append([(a, b)] + m)
        return out

    def far(m):
        return sum(0 if topo.same_plane(T.cores[a], T.cores[b]) else 1 for a, b in m)

    allm = sorted(matchings(list(range(N))), key=far)

    def pick(chosen, used):
        if len(chosen) == N - 1:
            return chosen
        for m in allm:
            if not any(e in used for e in m):
                r = pick(chosen + [m], used | set(m))
                if r:
                    return r
        return None

    chosen = sorted(pick([], set()), key=lambda m: -far(m))
    part = {}
    for t, m in enumerate(chosen):
        part[t + 1] = {}
        for a, b in m:
            part[t + 1][a] = b
            part[t + 1][b] = a
    return part


def rank_program(g, core, T, topo):
    rank = T.rank_of(core)
    if rank is None:
        return
    ACT, OP = ActivationFunctionType, AluOpType
    Q = {"g": g, "v": g.vector, "s": g.scalar, "t": g.tensor, "y": g.sync}
    cnt, seen = [0], {}
    part = rounds_of(T, topo)

    def ev():
        cnt[0] += 1
        return "e%d" % (cnt[0] - 1)

    def wait(qn, name, val=1):
        if seen.get((qn, name), 0) < val:
            seen[(qn, name)] = val
            Q[qn].wait_ge(T.sem[name], val)

    def engines(src):
        m = None
        for d in T.cores:
            if d != src:
                m = topo.mask(src, d) if m is None else m & topo.mask(src, d)
        return [e for e in range(m.bit_length()) if (m >> e) & 1]

    def share(n, src):
        k = 1
        while 2 * k * n <= len(engines(src)):
            k *= 2
        return k

    def bits(es):
        m = 0
        for e in es:
            m |= 1 << e
        return m

    PS = [T["ps%d" % b] for b in range(8)]
    readers = {b: [] for b in range(8)}

    def claim(b):
        for n_, v_ in readers[b]:
            wait("t", n_, v_)
        readers[b] = []
        return PS[b]

    ldq, ldd, ldk, ldv = ev(), ev(), ev(), ev()
    g.sync.dma_start(T.qraw[:, :], T.q[:, :]).then_inc(T.sem[ldq], 16)
    g.scalar.dma_start(T.qd[:, :], T.q[:, :]).then_inc(T.sem[ldd], 16)
    g.sync.dma_start(T.kk[:, :], T.k[:, :]).then_inc(T.sem[ldk], 16)
    g.sync.dma_start(T.vv[:, :], T.v[:, :]).then_inc(T.sem[ldv], 16)

    init, ninit = ev(), [0]

    def fill(ap, c):
        g.vector.memset(ap, c).then_inc(T.sem[init], 1)
        ninit[0] += 1

    eone, ezero = ev(), ev()
    g.vector.memset(T.ones[:, :], 1.0).then_inc(T.sem[eone], 1)
    fill(T.c256[:, :], 1.0 / 256.0)
    wait("s", eone)
    g.scalar.activation(T.msg[:, :, QP], T.ones[:, 0:N - 1], ACT.Sqrt, scale=0.0).then_inc(T.sem[ezero], 1)
    for i in range(NMAX):
        for j in range(NMAX):
            fill(T.mask[32 * i:32 * i + 32, j:j + 1], 1.0 if i == j else 0.0)
    NI = ninit[0]

    my = engines(core)
    sent = 0
    ids = {}
    for t in range(1, N):
        rid, pid = topo.addr(T.cores[part[t][rank]], core)
        ids[t] = DstId(rid=rid, pnc=pid)
    wait("g", ldd, 16)
    g.remote_dma_fused([RemoteDMATransfer(dst_ids=[ids[RAW]], dma_engine_mask=bits(my), remote_sem=T.sem["rw%d" % rank],
                                          srcs=[T.qd[:, :]], dsts=[T.ql[:, :]])], local_sem=T.sem.sent)
    sent += len(my)

    eqsq, exa, exb, esq, erx, eu, eqn, esc = ev(), ev(), ev(), ev(), ev(), ev(), ev(), ev()
    wait("v", init, NI)
    wait("v", ldq, 16)
    g.vector.tensor_tensor(T.qsq[:, :], T.qraw[:, :], T.qraw[:, :], OP.mult).then_inc(T.sem[eqsq], 1)
    wait("t", init, NI)
    wait("t", eone)
    wait("t", eqsq)
    g.tensor.matmul(PS[0][:, 0:QP], T.c256[:, :], T.qsq[:, :], True, True).then_inc(T.sem[exa], 1)
    g.tensor.matmul(PS[1][:, 0:QP], T.c256[:, :], T.qsq[:, :], True, True).then_inc(T.sem[exb], 1)
    wait("s", exa)
    g.scalar.activation(T.sq[:, :], PS[0][:, 0:QP], ACT.Sqrt).then_inc(T.sem[esq], 1)
    readers[0].append((esq, 1))
    wait("v", exb)
    g.vector.reciprocal(T.rx[:, :], PS[1][:, 0:QP]).then_inc(T.sem[erx], 1)
    readers[1].append((erx, 1))
    wait("v", erx)
    g.vector.tensor_tensor(T.u[:, :], T.qraw[:, :], T.rx[:, :], OP.mult).then_inc(T.sem[eu], 1)
    wait("v", eu)
    wait("v", esq)
    g.vector.tensor_tensor(T.qown[:, :], T.u[:, :], T.sq[:, :], OP.mult).then_inc(T.sem[eqn], 1)
    g.vector.tensor_tensor(T.sc[:, :], T.rx[:, :], T.sq[:, :], OP.mult).then_inc(T.sem[esc], 1)

    early = [t for t in range(1, N) if t != RAW]
    wait("g", eqn)
    g.remote_dma_fused([RemoteDMATransfer(dst_ids=[ids[t] for t in early], dma_engine_mask=bits(my),
                                          remote_sem=T.sem["qs%d" % rank], srcs=[T.qown[:, :]],
                                          dsts=[T.qall[:, QP * (t - 1):QP * t] for t in early])], local_sem=T.sem.sent)
    sent += len(my)
    wait("g", esc)
    g.remote_dma_fused([RemoteDMATransfer(dst_ids=[ids[RAW]], dma_engine_mask=bits(my), remote_sem=T.sem["qs%d" % rank],
                                          srcs=[T.sc[:, :]], dsts=[T.scl[:, :]])], local_sem=T.sem.sent)
    sent += len(my)
    eid = ev()
    wait("g", eone)
    g.affine_select(T.ident[:, :], T.ones[:, :], [[-1, 128]], OP.is_equal, 0.0, 0, 1).then_inc(T.sem[eid], 1)

    jr = part[RAW][rank]
    eld = ev()
    wait("y", "rw%d" % jr, len(engines(T.cores[jr])))
    g.sync.dma_start(T.qall[:, QP * (RAW - 1):QP * RAW], T.ql[:, :]).then_inc(T.sem[eld], 16)

    eksq, exk, esk, erk, eexp = ev(), ev(), ev(), ev(), ev()
    wait("s", ldk, 16)
    g.scalar.activation(T.ksq[:, :], T.kk[:, :], ACT.Square).then_inc(T.sem[eksq], 1)
    eS, eE = [ev(), ev()], [ev(), ev()]
    wait("t", eqn)
    wait("t", ldk, 16)
    for b in range(KB):
        g.tensor.matmul(PS[4 + b][:, 0:QP], T.kk[:, 128 * b:128 * b + 128], T.qown[:, :], True, True).then_inc(T.sem[eS[b]], 1)
    wait("t", eksq)
    for b in range(KB):
        g.tensor.matmul(PS[2][:, b:b + 1], T.ksq[:, 128 * b:128 * b + 128], T.ones[:, 0:1], True, True).then_inc(T.sem[exk], 1)
    wait("s", exk, KB)
    g.scalar.activation(T.sk[:, :], PS[2][:, 0:KB], ACT.Sqrt).then_inc(T.sem[esk], 1)
    readers[2].append((esk, 1))
    g.scalar.activation(T.onec[:, :], T.ones[:, 0:1], ACT.Exp, scale=0.0).then_inc(T.sem[eexp], 1)
    wait("v", esk)
    g.vector.reciprocal(T.rk[:, :], T.sk[:, :]).then_inc(T.sem[erk], 1)
    wait("s", erk)
    for b in range(KB):
        wait("s", eS[b])
        g.scalar.activation(T.P[:, b, 0:QP], PS[4 + b][:, 0:QP], ACT.Exp, bias=-16.0,
                            scale=T.rk[:, b:b + 1]).then_inc(T.sem[eE[b]], 1)
        readers[4 + b].append((eE[b], 1))
    eown = eE

    wait("t", ldv, 16)
    wait("t", eexp)
    st = {}

    def scores(gi):
        grp = GROUPS[gi]
        n, p0 = len(grp), grp[0]
        w = QP * n
        base = 4 * (gi % 2)
        raw = grp == [RAW]
        if raw:
            wait("t", eld, 16)
        else:
            for p in grp:
                j = part[p][rank]
                wait("t", "qs%d" % j, len(engines(T.cores[j])))
        eS, eE = [ev(), ev()], [ev(), ev()]
        for b in range(KB):
            S = claim(base + b)
            g.tensor.matmul(S[:, 0:w], T.kk[:, 128 * b:128 * b + 128], T.qall[:, QP * (p0 - 1):QP * (p0 - 1) + w],
                            True, True).then_inc(T.sem[eS[b]], 1)
        eM = [ev(), ev()] if raw else None
        if raw:
            wait("v", "qs%d" % jr, len(engines(T.cores[jr])))
            for b in range(KB):
                wait("v", eS[b])
                g.vector.tensor_tensor(T.Ssc[:, b, :], PS[base + b][:, 0:w], T.scl[:, :], OP.mult).then_inc(T.sem[eM[b]], 1)
                readers[base + b].append((eM[b], 1))
        for b in range(KB):
            if raw:
                wait("s", eM[b])
                src = T.Ssc[:, b, :]
            else:
                wait("s", eS[b])
                src = PS[base + b][:, 0:w]
            g.scalar.activation(T.P[:, b, QP * p0:QP * p0 + w], src, ACT.Exp, bias=-16.0,
                                scale=T.rk[:, b:b + 1]).then_inc(T.sem[eE[b]], 1)
            if not raw:
                readers[base + b].append((eE[b], 1))
        st[gi] = eE

    def parts(gi):
        grp = GROUPS[gi]
        n, p0 = len(grp), grp[0]
        w = QP * n
        base = 4 * (gi % 2)
        eE = st[gi]
        enum, eden, ecn, ecd = ev(), ev(), ev(), ev()
        NUM, DEN = claim(base + 2), claim(base + 3)
        for b in range(KB):
            wait("t", eE[b])
            Pb = T.P[:, b, QP * p0:QP * p0 + w]
            g.tensor.matmul(DEN[0:w, 0:1], Pb, T.onec[:, 0:1], b == 0, b == KB - 1).then_inc(T.sem[eden], 1)
            g.tensor.matmul(NUM[:, 0:w], T.vv[:, 128 * b:128 * b + 128], Pb, b == 0, b == KB - 1).then_inc(T.sem[enum], 1)
        if n == 1:
            wait("s", eden, KB)
            wait("s", ezero)
            g.scalar.activation(T.msg[0:QP, p0 - 1, QP:QP + 1], DEN[0:QP, 0:1], ACT.Copy).then_inc(T.sem[ecd], 1)
        wait("v", enum, KB)
        out = T.msg[:, p0 - 1, 0:QP] if n == 1 else T.msg[:, p0 - 1:p0 - 1 + n, 0:QP]
        g.vector.tensor_copy(out, NUM[:, 0:w]).then_inc(T.sem[ecn], 1)
        readers[base + 2].append((ecn, 1))
        if n > 1:
            wait("v", eden, KB)
            wait("v", ezero)
            g.vector.tensor_scalar(T.msg[0:w, p0 - 1:p0 - 1 + n, QP], T.mask[0:w, 0:n], DEN[0:w, 0:1], None,
                                   OP.mult).then_inc(T.sem[ecd], 1)
        readers[base + 3].append((ecd, 1))
        k = share(n, core)
        trs = []
        for i, p in enumerate(grp):
            trs.append(RemoteDMATransfer(dst_ids=[ids[p]], dma_engine_mask=bits(my[i * k:(i + 1) * k]),
                                         remote_sem=T.sem["ps%d" % p], srcs=[T.msg[:, p - 1, :]],
                                         dsts=[T.land[:, p - 1, :]]))
        wait("g", ecn)
        wait("g", ecd)
        g.remote_dma_fused(trs, local_sem=T.sem.sent)
        return k * n

    NG = len(GROUPS)
    for gi in range(NG - 2):
        scores(gi)
        sent += parts(gi)
    scores(NG - 2)
    scores(NG - 1)
    sent += parts(NG - 2)
    sent += parts(NG - 1)

    base = 4 * (len(GROUPS) % 2)
    H = 64
    YA, DA = [claim(base), claim(base + 2)], claim(base + 1)
    ey, ed, erd, eyt, est = [ev(), ev()], ev(), ev(), ev(), ev()
    for b in range(KB):
        wait("t", eown[b])
        g.tensor.matmul(DA[0:QP, 0:1], T.P[:, b, 0:QP], T.onec[:, 0:1], b == 0, False).then_inc(T.sem[ed], 1)
        for h in range(2):
            g.tensor.matmul(YA[h][0:QP, 0:H], T.P[:, b, 0:QP], T.vv[:, 128 * b + H * h:128 * b + H * h + H], b == 0,
                            False).then_inc(T.sem[ey[h]], 1)
    wait("t", eid)
    order = [(p, i, len(grp)) for grp in GROUPS for i, p in enumerate(grp)]
    for c, (p, i, n) in enumerate(order):
        last = c == len(order) - 1
        wait("t", "ps%d" % p, share(n, T.cores[part[p][rank]]))
        g.tensor.matmul(DA[0:QP, 0:1], T.ident[:, QP * i:QP * i + QP], T.land[:, p - 1, QP:QP + 1], False,
                        last).then_inc(T.sem[ed], 1)
        for h in range(2):
            g.tensor.matmul(YA[h][0:QP, 0:H], T.land[:, p - 1, 0:QP], T.ident[:, H * h:H * h + H], False,
                            last).then_inc(T.sem[ey[h]], 1)
    wait("v", ed, KB + N - 1)
    g.vector.reciprocal(T.rden[0:QP, :], DA[0:QP, 0:1]).then_inc(T.sem[erd], 1)
    wait("v", erd)
    wait("v", ey[0], KB + N - 1)
    g.vector.tensor_scalar(T.yt[0:QP, 0:H], YA[0][0:QP, 0:H], T.rden[0:QP, 0:1], None, OP.mult).then_inc(T.sem[eyt], 1)
    wait("s", erd)
    wait("s", ey[1], KB + N - 1)
    g.scalar.activation(T.yt[0:QP, H:2 * H], YA[1][0:QP, 0:H], ACT.Copy, scale=T.rden[0:QP, 0:1]).then_inc(T.sem[eyt], 1)
    wait("y", eyt, 2)
    g.sync.dma_start(T.y[:, :], T.yt[0:QP, :]).then_inc(T.sem[est], 16)
    wait("y", est, 16)
    wait("g", "sent", sent)
